import numpy as np
import ml_dtypes


def mxq(x, axis, fmt="e4m3"):
    dtype, down = {"e4m3": (ml_dtypes.float8_e4m3fn, 7), "e5m2": (ml_dtypes.float8_e5m2, 14)}[fmt]
    v = np.moveaxis(np.asarray(x, np.float32).astype(ml_dtypes.bfloat16).astype(np.float64), axis, -1)
    blocks = v.reshape(v.shape[:-1] + (-1, 32))
    amax = np.abs(blocks).max(-1, keepdims=True)
    byte = np.maximum(np.where(amax > 0, np.frexp(amax)[1] - 1 + 127, 0) - down, 1)
    scale = np.exp2(byte - 127.0)
    codes = (blocks / scale).astype(np.float32).astype(dtype).astype(np.float64)
    return np.moveaxis((codes * scale).reshape(v.shape), -1, axis)


WIDE = False


def mx_kscale(k):
    if not WIDE:
        return np.ones(k)
    levels = np.array([30, -30])
    if k % 512:
        return np.exp2(np.random.permutation(np.resize(levels, k // 32))).repeat(32)
    a = np.empty((k // 512, 16))
    for p in range(k // 512):
        a[p, :8] = np.random.permutation(np.resize(levels, 8))
        for g in range(8):
            far = levels[np.abs(levels - a[p, g]) >= 10]
            a[p, g + 8] = far[np.random.randint(len(far))]
    return np.exp2(a.ravel()).repeat(32)


def f64(x):
    return np.asarray(x).astype(np.float64)


def striped(idx):
    return np.tile(np.asarray(idx).reshape(-1, 16).T, (8, 1)).astype(np.uint16)


def unstriped(offs):
    return offs[:16].T.reshape(-1).astype(np.int64)


E2M1 = np.array([0.0, 0.5, 1.0, 1.5, 2.0, 3.0, 4.0, 6.0, -0.0, -0.5, -1.0, -1.5, -2.0, -3.0, -4.0, -6.0])


def pack_weight(w, fmt):
    k, n = w.shape
    w = f64(np.asarray(w, np.float32).astype(ml_dtypes.bfloat16)).reshape(k // 32, 32, n)
    amax = np.abs(w).max(1)
    if fmt == "e4m3":
        byte = np.frexp(amax)[1] - 1 + 127 - 7
    else:
        mant, ex = np.frexp(amax / 6.0)
        byte = np.where(mant > 0.5, ex, ex - 1) + 127
    byte = np.clip(np.where(amax > 0, byte, 1), 1, 254)
    scaled = (w * np.exp2(127.0 - byte)[:, None, :]).reshape(k, n).astype(np.float32)
    by_word = np.ascontiguousarray(scaled.reshape(k // 512, 128, 4, n).transpose(0, 1, 3, 2))
    if fmt == "e4m3":
        words = by_word.astype(ml_dtypes.float8_e4m3fn).view(np.uint8)
    else:
        c = by_word.astype(ml_dtypes.float4_e2m1fn).view(np.uint8) & 0xF
        words = (c[..., 0::2] | (c[..., 1::2] << 4)).reshape(k // 512, 128, 2 * n)
    return np.ascontiguousarray(words), np.ascontiguousarray(byte.astype(np.uint8).reshape(k // 512, 16, n))


def unpack_weight(words, scales, fmt):
    g, _, n = scales.shape
    words = np.ascontiguousarray(words).reshape(g, 128, n, -1)
    if fmt == "e4m3":
        vals = words.view(ml_dtypes.float8_e4m3fn).astype(np.float64)
    else:
        nib = np.empty((g, 128, n, 4), np.uint8)
        nib[..., 0::2] = words & 0xF
        nib[..., 1::2] = words >> 4
        vals = E2M1[nib]
    vals = vals * np.repeat(np.exp2(scales.astype(np.float64) - 127.0), 8, axis=1)[..., None]
    return vals.transpose(0, 1, 3, 2).reshape(g * 512, n)


N, K, T, J = 1024, 512, 1024, 512


def setup_inputs():
    n = np.random.standard_normal
    idx = np.random.permutation(T)[:J]
    fn = mx_kscale(N)
    wp = pack_weight(n((N, K)) * 1 / np.sqrt(N) * fn[:, None], "e2m1")
    return {
        "e": (n((N, T)) / fn[:, None]).astype(np.float32),
        "pr": (np.random.uniform(0.02, 0.98, (N, T))).astype(np.float32),
        "w_words": wp[0],
        "w_scales": wp[1],
        "run": (0.3 * n((K, T))).astype(np.float32),
        "offs": striped(idx),
    }


def reference(e, pr, w_words, w_scales, run, offs):
    idx = unstriped(offs)
    wu = unpack_weight(w_words, w_scales, "e2m1")
    d = f64(e)[:, idx] * np.square(1.0 - f64(pr)[:, idx])
    dq = mxq(d, 0, "e5m2")
    dx = wu.T @ dq
    p = np.zeros((K, T))
    p[:, idx] = dx
    y = p + f64(run)
    return y

@@ -1,0 +1,177 @@
+from contextlib import ExitStack
+
+import concourse.mybir as mybir
+from concourse.masks import make_identity
+
+N, K, T, J = 1024, 512, 1024, 512
+FLOPS = 2 * N * K * J
+
+F32 = mybir.dt.float32
+BF16 = mybir.dt.bfloat16
+I32 = mybir.dt.int32
+U32 = mybir.dt.uint32
+U16 = mybir.dt.uint16
+U8 = mybir.dt.uint8
+E5M2X4 = mybir.dt.float8_e5m2_x4
+E2M1X4 = mybir.dt.float4_e2m1fn_x4
+MULT = mybir.AluOpType.mult
+ADD = mybir.AluOpType.add
+SQUARE = mybir.ActivationFunctionType.Square
+
+P = 128
+PACK = 4
+PASSES = N // (P * PACK)
+PLANES = PASSES * PACK
+K_TILES = K // P
+BANK = 512
+LANES = 16
+CHUNKS = ([(0, J)], [(0, J // 2), (J // 2, J)])
+
+
+def tile_list_confidence_weighted_back_kernel(tc, e, pr, w_words, w_scales, run, offs, out):
+    nc = tc.nc
+    with ExitStack() as ctx:
+        keep = ctx.enter_context(tc.tile_pool(name="keep", bufs=1))
+        acc_pool = ctx.enter_context(tc.psum_pool(name="acc", bufs=6))
+        back_pool = ctx.enter_context(tc.psum_pool(name="back", bufs=2))
+
+        offsets = keep.tile([P, J // LANES], U16, name="offsets")
+        nc.sync.dma_start(offsets[:], offs)
+
+        e_rows = e.rearrange("(z p r) t -> z r p t", p=P, r=PACK)
+        pr_rows = pr.rearrange("(z p r) t -> z r p t", p=P, r=PACK)
+        e_sb = [keep.tile([P, T], F32, name="e%d" % m) for m in range(PLANES)]
+        pr_sb = [keep.tile([P, T], F32, name="pr%d" % m) for m in range(PLANES)]
+        w_sb = [keep.tile([P, 2 * K], U8, name="w%d" % z, align_bytes=64) for z in range(PASSES)]
+        ws_sb = keep.tile([P, PASSES, K], U8, name="ws", align_bytes=64)
+        run_sb = [keep.tile([P, T], F32, name="run%d" % i) for i in range(K_TILES)]
+        page = [keep.tile([P, T], F32, name="page%d" % i) for i in range(K_TILES)]
+        ident = keep.tile([P, P], F32, name="ident")
+
+        nc.vector.memset(ws_sb[:].rearrange("p z c -> p (z c)").bitcast(I32), 0)
+        for i in range(K_TILES):
+            nc.vector.memset(page[i][:], 0.0)
+        make_identity(nc, ident[:])
+
+        def load_e(m):
+            nc.sync.dma_start(e_sb[m][:], e_rows[m // PACK, m % PACK])
+
+        def load_pr(m):
+            nc.sync.dma_start(pr_sb[m][:], pr_rows[m // PACK, m % PACK])
+
+        def load_w(z):
+            nc.sync.dma_start(w_sb[z][:].bitcast(I32), w_words[z].bitcast(I32))
+
+        load_pr(0)
+        for m in range(PLANES):
+            if m + 1 < PLANES:
+                load_pr(m + 1)
+            load_e(m)
+            if m == 0:
+                for q in range(4):
+                    nc.sync.dma_start(
+                        ws_sb[32 * q : 32 * q + 4, :, :].bitcast(I32),
+                        w_scales[:, 4 * q : 4 * q + 4, :].rearrange("z r c -> r z c").bitcast(I32),
+                    )
+            if m % PACK == PACK - 1:
+                load_w(m // PACK)
+        for i in range(K_TILES):
+            nc.sync.dma_start(run_sb[i][:], run[i * P : (i + 1) * P, :])
+
+        doubt = [keep.tile([P, J], F32, name="doubt%d" % m) for m in range(PLANES)]
+
+        def make_doubt(m):
+            picked = keep.tile([P, J], F32, name="picked%d" % m)
+            nc.vector.tensor_copy(picked[:], pr_sb[m][:].indirect(offsets[:]))
+            nc.scalar.activation(doubt[m][:], picked[:], SQUARE, bias=1.0, scale=-1.0)
+
+        d_codes = [keep.tile([P, J], U32, name="dc%d" % z, align_bytes=64) for z in range(PASSES)]
+        d_scales = [keep.tile([P, J], U8, name="ds%d" % z, align_bytes=64) for z in range(PASSES)]
+        d = [
+            [keep.tile([P, PACK, b - a], F32, name="d%d_%d" % (z, a)) for a, b in CHUNKS[z]]
+            for z in range(PASSES)
+        ]
+        acc = [acc_pool.tile([P, BANK], F32, name="acc%d" % i, tag="acc") for i in range(K_TILES)]
+
+        make_doubt(0)
+        for m in range(PLANES):
+            z, r = divmod(m, PACK)
+            if m + 1 < PLANES:
+                make_doubt(m + 1)
+            for c, (a, b) in enumerate(CHUNKS[z]):
+                nc.vector.tensor_tensor(
+                    d[z][c][:, r, :],
+                    e_sb[m][:].indirect(offsets[:, a // LANES : b // LANES]),
+                    doubt[m][:, a:b],
+                    MULT,
+                )
+            if r == PACK - 1:
+                woven = []
+                for c, (a, b) in enumerate(CHUNKS[z]):
+                    wv = keep.tile([P, b - a, PACK], BF16, name="wv%d_%d" % (z, a), align_bytes=64)
+                    dst = wv[:].rearrange("p (c i) r -> p c r i", i=4)
+                    src = d[z][c][:].rearrange("p r (c i) -> p c r i", i=4)
+                    if c == 0:
+                        nc.scalar.copy(dst, src)
+                    else:
+                        nc.vector.tensor_copy(dst, src)
+                    woven.append(wv)
+                for c, (a, b) in enumerate(CHUNKS[z]):
+                    nc.vector.quantize_mx(
+                        out=d_codes[z][:, a:b].bitcast(E5M2X4),
+                        scales=d_scales[z][:, a:b],
+                        in_=woven[c][:].rearrange("p j r -> p (j r)"),
+                    )
+                for i in range(K_TILES):
+                    nc.tensor.matmul_mx(
+                        out=acc[i][:],
+                        lhsT=w_sb[z][:, 2 * P * i : 2 * P * (i + 1)].bitcast(E2M1X4),
+                        lhsT_scale=ws_sb[:, z, P * i : P * (i + 1)],
+                        rhs=d_codes[z][:].bitcast(E5M2X4),
+                        rhs_scale=d_scales[z][:],
+                        start=(z == 0),
+                        stop=(z == PASSES - 1),
+                    )
+
+        dx = [keep.tile([P, J], F32, name="dx%d" % i) for i in range(K_TILES)]
+        for i in range(K_TILES):
+            nc.scalar.copy(dx[i][:], acc[i][:])
+
+        blocks = BANK // P
+        halves = T // BANK
+
+        def turn(dst, src, first, last):
+            for b in range(blocks):
+                nc.tensor.matmul(
+                    dst[:, b * P : (b + 1) * P],
+                    lhsT=src[:, b * P : (b + 1) * P],
+                    rhs=ident[:],
+                    is_transpose=True,
+                    start=(first and b == 0),
+                    stop=(last and b == blocks - 1),
+                )
+
+        turned = {}
+        for i in range(K_TILES - 1):
+            for h in range(halves):
+                turned[i, h] = acc_pool.tile([P, BANK], F32, name="turned", tag="acc")
+                turn(turned[i, h], run_sb[i][:, h * BANK : (h + 1) * BANK], True, False)
+
+        for i in range(K_TILES):
+            nc.vector.tensor_copy(page[i][:].indirect(offsets[:]), dx[i][:])
+            y = [keep.tile([P, BANK], F32, name="y%d_%d" % (i, h)) for h in range(halves)]
+            if i == K_TILES - 1:
+                for h in range(halves):
+                    cols = slice(h * BANK, (h + 1) * BANK)
+                    nc.vector.tensor_tensor(y[h][:], page[i][:, cols], run_sb[i][:, cols], ADD)
+            else:
+                sums = [keep.tile([P, BANK], F32, name="ts%d_%d" % (i, h)) for h in range(halves)]
+                for h in range(halves):
+                    turn(turned[i, h], page[i][:, h * BANK : (h + 1) * BANK], False, True)
+                    nc.scalar.copy(sums[h][:], turned[i, h][:])
+                for h in range(halves):
+                    back = back_pool.tile([P, BANK], F32, name="back")
+                    turn(back, sums[h], True, True)
+                    nc.scalar.copy(y[h][:], back[:])
+            for h in range(halves):
+                nc.sync.dma_start(out[i * P : (i + 1) * P, h * BANK : (h + 1) * BANK], y[h][:])

@@ -25,14 +25,15 @@ PLANES = PASSES * PACK
 K_TILES = K // P
 BANK = 512
 LANES = 16
-CHUNKS = ([(0, J)], [(0, J // 2), (J // 2, J)])
+CHUNK = 128
 
 
 def tile_list_confidence_weighted_back_kernel(tc, e, pr, w_words, w_scales, run, offs, out):
     nc = tc.nc
     with ExitStack() as ctx:
         keep = ctx.enter_context(tc.tile_pool(name="keep", bufs=1))
-        acc_pool = ctx.enter_context(tc.psum_pool(name="acc", bufs=6))
+        acc_pool = ctx.enter_context(tc.psum_pool(name="acc", bufs=4))
+        turn_pool = ctx.enter_context(tc.psum_pool(name="turn", bufs=2))
         back_pool = ctx.enter_context(tc.psum_pool(name="back", bufs=2))
 
         offsets = keep.tile([P, J // LANES], U16, name="offsets")
@@ -49,9 +50,9 @@ def tile_list_confidence_weighted_back_kernel(tc, e, pr, w_words, w_scales, run,
         ident = keep.tile([P, P], F32, name="ident")
 
         nc.vector.memset(ws_sb[:].rearrange("p z c -> p (z c)").bitcast(I32), 0)
-        for i in range(K_TILES):
-            nc.vector.memset(page[i][:], 0.0)
         make_identity(nc, ident[:])
+        for i in range(K_TILES):
+            (nc.vector if i < 2 else nc.gpsimd).memset(page[i][:], 0.0)
 
         def load_e(m):
             nc.sync.dma_start(e_sb[m][:], e_rows[m // PACK, m % PACK])
@@ -87,51 +88,67 @@ def tile_list_confidence_weighted_back_kernel(tc, e, pr, w_words, w_scales, run,
 
         d_codes = [keep.tile([P, J], U32, name="dc%d" % z, align_bytes=64) for z in range(PASSES)]
         d_scales = [keep.tile([P, J], U8, name="ds%d" % z, align_bytes=64) for z in range(PASSES)]
-        d = [
-            [keep.tile([P, PACK, b - a], F32, name="d%d_%d" % (z, a)) for a, b in CHUNKS[z]]
-            for z in range(PASSES)
-        ]
         acc = [acc_pool.tile([P, BANK], F32, name="acc%d" % i, tag="acc") for i in range(K_TILES)]
 
+        def product(m, dst):
+            nc.vector.tensor_tensor(dst, e_sb[m][:].indirect(offsets[:]), doubt[m][:], MULT)
+
+        def quantize(z, a, woven):
+            b = a + woven.shape[1]
+            nc.vector.quantize_mx(
+                out=d_codes[z][:, a:b].bitcast(E5M2X4),
+                scales=d_scales[z][:, a:b],
+                in_=woven[:].rearrange("p j r -> p (j r)"),
+            )
+
+        def multiply(z):
+            for i in range(K_TILES):
+                nc.tensor.matmul_mx(
+                    out=acc[i][:],
+                    lhsT=w_sb[z][:, 2 * P * i : 2 * P * (i + 1)].bitcast(E2M1X4),
+                    lhsT_scale=ws_sb[:, z, P * i : P * (i + 1)],
+                    rhs=d_codes[z][:].bitcast(E5M2X4),
+                    rhs_scale=d_scales[z][:],
+                    start=(z == 0),
+                    stop=(z == PASSES - 1),
+                )
+
+        d_first = keep.tile([P, PACK, J], F32, name="d_first")
         make_doubt(0)
-        for m in range(PLANES):
-            z, r = divmod(m, PACK)
-            if m + 1 < PLANES:
-                make_doubt(m + 1)
-            for c, (a, b) in enumerate(CHUNKS[z]):
+        for m in range(PACK):
+            make_doubt(m + 1)
+            product(m, d_first[:, m, :])
+        woven_first = keep.tile([P, J, PACK], BF16, name="woven_first", align_bytes=64)
+        nc.scalar.copy(
+            woven_first[:].rearrange("p (c i) r -> p c r i", i=4),
+            d_first[:].rearrange("p r (c i) -> p c r i", i=4),
+        )
+        quantize(0, 0, woven_first)
+        multiply(0)
+
+        d_low = keep.tile([P, 2, J], F32, name="d_low")
+        for m in range(PACK, PACK + 2):
+            make_doubt(m + 1)
+            product(m, d_low[:, m - PACK, :])
+        make_doubt(PLANES - 1)
+        starts = range(0, J, CHUNK)
+        woven = [keep.tile([P, CHUNK, PACK], BF16, name="woven%d" % a, align_bytes=64) for a in starts]
+        d_high = [keep.tile([P, 2, CHUNK], F32, name="d_high%d" % a) for a in starts]
+        for c, a in enumerate(starts):
+            nc.scalar.copy(woven[c][:, :, 0:2], d_low[:, :, a : a + CHUNK].rearrange("p r j -> p j r"))
+        for r in range(2):
+            m = PLANES - 2 + r
+            for c, a in enumerate(starts):
                 nc.vector.tensor_tensor(
-                    d[z][c][:, r, :],
-                    e_sb[m][:].indirect(offsets[:, a // LANES : b // LANES]),
-                    doubt[m][:, a:b],
+                    d_high[c][:, r, :],
+                    e_sb[m][:].indirect(offsets[:, a // LANES : (a + CHUNK) // LANES]),
+                    doubt[m][:, a : a + CHUNK],
                     MULT,
                 )
-            if r == PACK - 1:
-                woven = []
-                for c, (a, b) in enumerate(CHUNKS[z]):
-                    wv = keep.tile([P, b - a, PACK], BF16, name="wv%d_%d" % (z, a), align_bytes=64)
-                    dst = wv[:].rearrange("p (c i) r -> p c r i", i=4)
-                    src = d[z][c][:].rearrange("p r (c i) -> p c r i", i=4)
-                    if c == 0:
-                        nc.scalar.copy(dst, src)
-                    else:
-                        nc.vector.tensor_copy(dst, src)
-                    woven.append(wv)
-                for c, (a, b) in enumerate(CHUNKS[z]):
-                    nc.vector.quantize_mx(
-                        out=d_codes[z][:, a:b].bitcast(E5M2X4),
-                        scales=d_scales[z][:, a:b],
-                        in_=woven[c][:].rearrange("p j r -> p (j r)"),
-                    )
-                for i in range(K_TILES):
-                    nc.tensor.matmul_mx(
-                        out=acc[i][:],
-                        lhsT=w_sb[z][:, 2 * P * i : 2 * P * (i + 1)].bitcast(E2M1X4),
-                        lhsT_scale=ws_sb[:, z, P * i : P * (i + 1)],
-                        rhs=d_codes[z][:].bitcast(E5M2X4),
-                        rhs_scale=d_scales[z][:],
-                        start=(z == 0),
-                        stop=(z == PASSES - 1),
-                    )
+        for c, a in enumerate(starts):
+            nc.scalar.copy(woven[c][:, :, 2:4], d_high[c][:].rearrange("p r j -> p j r"))
+            quantize(1, a, woven[c])
+        multiply(1)
 
         dx = [keep.tile([P, J], F32, name="dx%d" % i) for i in range(K_TILES)]
         for i in range(K_TILES):
@@ -151,27 +168,26 @@ def tile_list_confidence_weighted_back_kernel(tc, e, pr, w_words, w_scales, run,
                     stop=(last and b == blocks - 1),
                 )
 
-        turned = {}
-        for i in range(K_TILES - 1):
-            for h in range(halves):
-                turned[i, h] = acc_pool.tile([P, BANK], F32, name="turned", tag="acc")
-                turn(turned[i, h], run_sb[i][:, h * BANK : (h + 1) * BANK], True, False)
-
         for i in range(K_TILES):
             nc.vector.tensor_copy(page[i][:].indirect(offsets[:]), dx[i][:])
-            y = [keep.tile([P, BANK], F32, name="y%d_%d" % (i, h)) for h in range(halves)]
+            rows = slice(i * P, (i + 1) * P)
             if i == K_TILES - 1:
                 for h in range(halves):
                     cols = slice(h * BANK, (h + 1) * BANK)
-                    nc.vector.tensor_tensor(y[h][:], page[i][:, cols], run_sb[i][:, cols], ADD)
+                    y_half = keep.tile([P, BANK], F32, name="y_half%d" % h)
+                    nc.vector.tensor_tensor(y_half[:], page[i][:, cols], run_sb[i][:, cols], ADD)
+                    nc.sync.dma_start(out[rows, cols], y_half[:])
             else:
+                y = keep.tile([P, T], F32, name="y%d" % i)
                 sums = [keep.tile([P, BANK], F32, name="ts%d_%d" % (i, h)) for h in range(halves)]
+                turned = [turn_pool.tile([P, BANK], F32, name="turned") for h in range(halves)]
                 for h in range(halves):
-                    turn(turned[i, h], page[i][:, h * BANK : (h + 1) * BANK], False, True)
-                    nc.scalar.copy(sums[h][:], turned[i, h][:])
+                    turn(turned[h], run_sb[i][:, h * BANK : (h + 1) * BANK], True, False)
+                for h in range(halves):
+                    turn(turned[h], page[i][:, h * BANK : (h + 1) * BANK], False, True)
+                    nc.scalar.copy(sums[h][:], turned[h][:])
                 for h in range(halves):
                     back = back_pool.tile([P, BANK], F32, name="back")
                     turn(back, sums[h], True, True)
-                    nc.scalar.copy(y[h][:], back[:])
-            for h in range(halves):
-                nc.sync.dma_start(out[i * P : (i + 1) * P, h * BANK : (h + 1) * BANK], y[h][:])
+                    nc.scalar.copy(y[:, h * BANK : (h + 1) * BANK], back[:])
+                nc.scalar.dma_start(out[rows, :], y[:])

@@ -1,7 +1,6 @@
 from contextlib import ExitStack
 
 import concourse.mybir as mybir
-from concourse.masks import make_identity
 
 N, K, T, J = 1024, 512, 1024, 512
 FLOPS = 2 * N * K * J
@@ -23,21 +22,22 @@ PACK = 4
 PASSES = N // (P * PACK)
 PLANES = PASSES * PACK
 K_TILES = K // P
-BANK = 512
 LANES = 16
-CHUNK = 128
+HALF = J // 2
+QUARTER = J // 4
 
 
 def tile_list_confidence_weighted_back_kernel(tc, e, pr, w_words, w_scales, run, offs, out):
     nc = tc.nc
     with ExitStack() as ctx:
         keep = ctx.enter_context(tc.tile_pool(name="keep", bufs=1))
-        acc_pool = ctx.enter_context(tc.psum_pool(name="acc", bufs=4))
-        turn_pool = ctx.enter_context(tc.psum_pool(name="turn", bufs=2))
-        back_pool = ctx.enter_context(tc.psum_pool(name="back", bufs=2))
+        psum = ctx.enter_context(tc.psum_pool(name="psum", bufs=1))
 
         offsets = keep.tile([P, J // LANES], U16, name="offsets")
         nc.sync.dma_start(offsets[:], offs)
+
+        def entries(a, b):
+            return offsets[:, a // LANES : b // LANES]
 
         e_rows = e.rearrange("(z p r) t -> z r p t", p=P, r=PACK)
         pr_rows = pr.rearrange("(z p r) t -> z r p t", p=P, r=PACK)
@@ -47,10 +47,12 @@ def tile_list_confidence_weighted_back_kernel(tc, e, pr, w_words, w_scales, run,
         ws_sb = keep.tile([P, PASSES, K], U8, name="ws", align_bytes=64)
         run_sb = [keep.tile([P, T], F32, name="run%d" % i) for i in range(K_TILES)]
         page = [keep.tile([P, T], F32, name="page%d" % i) for i in range(K_TILES)]
-        ident = keep.tile([P, P], F32, name="ident")
+        codes = keep.tile([P, HALF + PASSES * J], U32, name="codes", align_bytes=64)
+        scales = keep.tile([P, HALF + PASSES * J], U8, name="scales", align_bytes=64)
 
         nc.vector.memset(ws_sb[:].rearrange("p z c -> p (z c)").bitcast(I32), 0)
-        make_identity(nc, ident[:])
+        nc.vector.memset(codes[:, 0:HALF], 0)
+        nc.vector.memset(scales[:, 0:HALF].bitcast(I32), 0)
         for i in range(K_TILES):
             (nc.vector if i < 2 else nc.gpsimd).memset(page[i][:], 0.0)
 
@@ -59,9 +61,6 @@ def tile_list_confidence_weighted_back_kernel(tc, e, pr, w_words, w_scales, run,
 
         def load_pr(m):
             nc.sync.dma_start(pr_sb[m][:], pr_rows[m // PACK, m % PACK])
-
-        def load_w(z):
-            nc.sync.dma_start(w_sb[z][:].bitcast(I32), w_words[z].bitcast(I32))
 
         load_pr(0)
         for m in range(PLANES):
@@ -75,119 +74,123 @@ def tile_list_confidence_weighted_back_kernel(tc, e, pr, w_words, w_scales, run,
                         w_scales[:, 4 * q : 4 * q + 4, :].rearrange("z r c -> r z c").bitcast(I32),
                     )
             if m % PACK == PACK - 1:
-                load_w(m // PACK)
+                nc.sync.dma_start(w_sb[m // PACK][:].bitcast(I32), w_words[m // PACK].bitcast(I32))
         for i in range(K_TILES):
             nc.sync.dma_start(run_sb[i][:], run[i * P : (i + 1) * P, :])
 
-        doubt = [keep.tile([P, J], F32, name="doubt%d" % m) for m in range(PLANES)]
+        picked = [keep.tile([P, J], F32, name="picked%d" % m) for m in range(PLANES)]
 
-        def make_doubt(m):
-            picked = keep.tile([P, J], F32, name="picked%d" % m)
-            nc.vector.tensor_copy(picked[:], pr_sb[m][:].indirect(offsets[:]))
-            nc.scalar.activation(doubt[m][:], picked[:], SQUARE, bias=1.0, scale=-1.0)
+        def pick(m):
+            nc.vector.tensor_copy(picked[m][:], pr_sb[m][:].indirect(offsets[:]))
 
-        d_codes = [keep.tile([P, J], U32, name="dc%d" % z, align_bytes=64) for z in range(PASSES)]
-        d_scales = [keep.tile([P, J], U8, name="ds%d" % z, align_bytes=64) for z in range(PASSES)]
-        acc = [acc_pool.tile([P, BANK], F32, name="acc%d" % i, tag="acc") for i in range(K_TILES)]
+        def fade(dst, src):
+            nc.scalar.activation(dst, src, SQUARE, bias=1.0, scale=-1.0)
 
-        def product(m, dst):
-            nc.vector.tensor_tensor(dst, e_sb[m][:].indirect(offsets[:]), doubt[m][:], MULT)
+        def product(dst, m, a, b, doubt):
+            nc.vector.tensor_tensor(dst, e_sb[m][:].indirect(entries(a, b)), doubt, MULT)
+
+        def weave_pair(woven, r, pair):
+            nc.scalar.copy(woven[:, :, r : r + 2], pair.rearrange("p r j -> p j r"))
 
         def quantize(z, a, woven):
-            b = a + woven.shape[1]
+            c0 = HALF + z * J + a
+            c1 = c0 + woven.shape[1]
             nc.vector.quantize_mx(
-                out=d_codes[z][:, a:b].bitcast(E5M2X4),
-                scales=d_scales[z][:, a:b],
+                out=codes[:, c0:c1].bitcast(E5M2X4),
+                scales=scales[:, c0:c1],
                 in_=woven[:].rearrange("p j r -> p (j r)"),
             )
 
-        def multiply(z):
-            for i in range(K_TILES):
-                nc.tensor.matmul_mx(
-                    out=acc[i][:],
-                    lhsT=w_sb[z][:, 2 * P * i : 2 * P * (i + 1)].bitcast(E2M1X4),
-                    lhsT_scale=ws_sb[:, z, P * i : P * (i + 1)],
-                    rhs=d_codes[z][:].bitcast(E5M2X4),
-                    rhs_scale=d_scales[z][:],
-                    start=(z == 0),
-                    stop=(z == PASSES - 1),
-                )
+        def multiply(dst, i, z, c0):
+            nc.tensor.matmul_mx(
+                out=dst[:],
+                lhsT=w_sb[z][:, 2 * P * i : 2 * P * (i + 1)].bitcast(E2M1X4),
+                lhsT_scale=ws_sb[:, z, P * i : P * (i + 1)],
+                rhs=codes[:, c0 : c0 + J].bitcast(E5M2X4),
+                rhs_scale=scales[:, c0 : c0 + J],
+                start=(z == 0),
+                stop=(z == PASSES - 1),
+            )
 
+        acc = [psum.tile([P, J], F32, name="acc%d" % i) for i in range(K_TILES)]
+        early = psum.tile([P, J], F32, name="early")
+        dx = [keep.tile([P, J], F32, name="dx%d" % i) for i in range(1, K_TILES)]
+        dx_first = [keep.tile([P, HALF], F32, name="dx0_%d" % h) for h in range(2)]
+
+        doubt = [keep.tile([P, J], F32, name="doubt%d" % m, tag="doubt%d" % m) for m in range(PLANES - 1)]
+        last_a = keep.tile([P, HALF], F32, name="last_a", tag="last_a")
+        last_b = keep.tile([P, HALF], F32, name="last_b")
         d_first = keep.tile([P, PACK, J], F32, name="d_first")
-        make_doubt(0)
+        pick(0)
+        fade(doubt[0][:], picked[0][:])
         for m in range(PACK):
-            make_doubt(m + 1)
-            product(m, d_first[:, m, :])
+            pick(m + 1)
+            fade(doubt[m + 1][:], picked[m + 1][:])
+            product(d_first[:, m, :], m, 0, J, doubt[m][:])
+
+        d_a = [keep.tile([P, 2, HALF], F32, name="d_a%d" % u) for u in range(2)]
+        woven_a = keep.tile([P, HALF, PACK], BF16, name="woven_a", align_bytes=64)
         woven_first = keep.tile([P, J, PACK], BF16, name="woven_first", align_bytes=64)
-        nc.scalar.copy(
-            woven_first[:].rearrange("p (c i) r -> p c r i", i=4),
-            d_first[:].rearrange("p r (c i) -> p c r i", i=4),
-        )
-        quantize(0, 0, woven_first)
-        multiply(0)
+        for r in range(PACK):
+            m = PACK + r
+            if m + 1 < PLANES - 1:
+                pick(m + 1)
+                fade(doubt[m + 1][:], picked[m + 1][:])
+            elif m + 1 == PLANES - 1:
+                pick(m + 1)
+                fade(last_a[:], picked[m + 1][:, 0:HALF])
+                fade(last_b[:], picked[m + 1][:, HALF:J])
+            product(d_a[r // 2][:, r % 2, :], m, 0, HALF, last_a[:] if m == PLANES - 1 else doubt[m][:, 0:HALF])
+            if r % 2 == 1:
+                weave_pair(woven_a, r - 1, d_a[r // 2][:])
+            if r == 0:
+                for h in range(2):
+                    nc.scalar.copy(
+                        woven_first[:, h * HALF : (h + 1) * HALF, :].rearrange("p (c i) r -> p c r i", i=4),
+                        d_first[:, :, h * HALF : (h + 1) * HALF].rearrange("p r (c i) -> p c r i", i=4),
+                    )
+                quantize(0, 0, woven_first)
+                multiply(early, 0, 0, 0)
+                for i in range(K_TILES):
+                    multiply(acc[i], i, 0, HALF)
+        quantize(1, 0, woven_a)
+        multiply(early, 0, 1, J)
+        nc.scalar.copy(dx_first[0][:], early[:, HALF:J])
 
-        d_low = keep.tile([P, 2, J], F32, name="d_low")
-        for m in range(PACK, PACK + 2):
-            make_doubt(m + 1)
-            product(m, d_low[:, m - PACK, :])
-        make_doubt(PLANES - 1)
-        starts = range(0, J, CHUNK)
-        woven = [keep.tile([P, CHUNK, PACK], BF16, name="woven%d" % a, align_bytes=64) for a in starts]
-        d_high = [keep.tile([P, 2, CHUNK], F32, name="d_high%d" % a) for a in starts]
-        for c, a in enumerate(starts):
-            nc.scalar.copy(woven[c][:, :, 0:2], d_low[:, :, a : a + CHUNK].rearrange("p r j -> p j r"))
+        d_low = keep.tile([P, 2, HALF], F32, name="d_low", tag="last_a")
+        woven_b = [keep.tile([P, QUARTER, PACK], BF16, name="woven_b%d" % c, align_bytes=64) for c in range(2)]
         for r in range(2):
-            m = PLANES - 2 + r
-            for c, a in enumerate(starts):
-                nc.vector.tensor_tensor(
-                    d_high[c][:, r, :],
-                    e_sb[m][:].indirect(offsets[:, a // LANES : (a + CHUNK) // LANES]),
-                    doubt[m][:, a : a + CHUNK],
-                    MULT,
-                )
-        for c, a in enumerate(starts):
-            nc.scalar.copy(woven[c][:, :, 2:4], d_high[c][:].rearrange("p r j -> p j r"))
-            quantize(1, a, woven[c])
-        multiply(1)
-
-        dx = [keep.tile([P, J], F32, name="dx%d" % i) for i in range(K_TILES)]
+            product(d_low[:, r, :], PACK + r, HALF, J, doubt[PACK + r][:, HALF:J])
+        for c in range(2):
+            weave_pair(woven_b[c], 0, d_low[:, :, c * QUARTER : (c + 1) * QUARTER])
+        for c in range(2):
+            a = HALF + c * QUARTER
+            d_high = keep.tile([P, 2, QUARTER], F32, name="d_high%d" % c, tag="doubt%d" % (PACK + c))
+            product(d_high[:, 0, :], PLANES - 2, a, a + QUARTER, doubt[PLANES - 2][:, a : a + QUARTER])
+            product(d_high[:, 1, :], PLANES - 1, a, a + QUARTER, last_b[:, c * QUARTER : (c + 1) * QUARTER])
+            weave_pair(woven_b[c], 2, d_high[:])
+        for c in range(2):
+            quantize(1, HALF + c * QUARTER, woven_b[c])
         for i in range(K_TILES):
-            nc.scalar.copy(dx[i][:], acc[i][:])
-
-        blocks = BANK // P
-        halves = T // BANK
-
-        def turn(dst, src, first, last):
-            for b in range(blocks):
-                nc.tensor.matmul(
-                    dst[:, b * P : (b + 1) * P],
-                    lhsT=src[:, b * P : (b + 1) * P],
-                    rhs=ident[:],
-                    is_transpose=True,
-                    start=(first and b == 0),
-                    stop=(last and b == blocks - 1),
-                )
+            multiply(acc[i], i, 1, HALF + J)
+        nc.scalar.copy(dx_first[1][:], acc[0][:, HALF:J])
+        for i in range(1, K_TILES):
+            nc.scalar.copy(dx[i - 1][:], acc[i][:])
 
         for i in range(K_TILES):
-            nc.vector.tensor_copy(page[i][:].indirect(offsets[:]), dx[i][:])
             rows = slice(i * P, (i + 1) * P)
+            if i == 0:
+                for h in range(2):
+                    nc.vector.tensor_copy(page[0][:].indirect(entries(h * HALF, (h + 1) * HALF)), dx_first[h][:])
+            else:
+                nc.vector.tensor_copy(page[i][:].indirect(offsets[:]), dx[i - 1][:])
             if i == K_TILES - 1:
-                for h in range(halves):
-                    cols = slice(h * BANK, (h + 1) * BANK)
-                    y_half = keep.tile([P, BANK], F32, name="y_half%d" % h)
+                for h in range(2):
+                    cols = slice(h * T // 2, (h + 1) * T // 2)
+                    y_half = keep.tile([P, T // 2], F32, name="y_half%d" % h)
                     nc.vector.tensor_tensor(y_half[:], page[i][:, cols], run_sb[i][:, cols], ADD)
                     nc.sync.dma_start(out[rows, cols], y_half[:])
             else:
                 y = keep.tile([P, T], F32, name="y%d" % i)
-                sums = [keep.tile([P, BANK], F32, name="ts%d_%d" % (i, h)) for h in range(halves)]
-                turned = [turn_pool.tile([P, BANK], F32, name="turned") for h in range(halves)]
-                for h in range(halves):
-                    turn(turned[h], run_sb[i][:, h * BANK : (h + 1) * BANK], True, False)
-                for h in range(halves):
-                    turn(turned[h], page[i][:, h * BANK : (h + 1) * BANK], False, True)
-                    nc.scalar.copy(sums[h][:], turned[h][:])
-                for h in range(halves):
-                    back = back_pool.tile([P, BANK], F32, name="back")
-                    turn(back, sums[h], True, True)
-                    nc.scalar.copy(y[:, h * BANK : (h + 1) * BANK], back[:])
+                nc.gpsimd.tensor_tensor(y[:], page[i][:], run_sb[i][:], ADD)
                 nc.scalar.dma_start(out[rows, :], y[:])

@@ -41,20 +41,18 @@ def tile_list_confidence_weighted_back_kernel(tc, e, pr, w_words, w_scales, run,
 
         e_rows = e.rearrange("(z p r) t -> z r p t", p=P, r=PACK)
         pr_rows = pr.rearrange("(z p r) t -> z r p t", p=P, r=PACK)
-        e_sb = [keep.tile([P, T], F32, name="e%d" % m) for m in range(PLANES)]
+        e_sb = [keep.tile([P, T], F32, name="e%d" % m, tag="e%d" % m, align_bytes=64) for m in range(PLANES)]
         pr_sb = [keep.tile([P, T], F32, name="pr%d" % m) for m in range(PLANES)]
         w_sb = [keep.tile([P, 2 * K], U8, name="w%d" % z, align_bytes=64) for z in range(PASSES)]
         ws_sb = keep.tile([P, PASSES, K], U8, name="ws", align_bytes=64)
         run_sb = [keep.tile([P, T], F32, name="run%d" % i) for i in range(K_TILES)]
         page = [keep.tile([P, T], F32, name="page%d" % i) for i in range(K_TILES)]
-        codes = keep.tile([P, HALF + PASSES * J], U32, name="codes", align_bytes=64)
         scales = keep.tile([P, HALF + PASSES * J], U8, name="scales", align_bytes=64)
 
-        nc.vector.memset(ws_sb[:].rearrange("p z c -> p (z c)").bitcast(I32), 0)
-        nc.vector.memset(codes[:, 0:HALF], 0)
-        nc.vector.memset(scales[:, 0:HALF].bitcast(I32), 0)
+        nc.gpsimd.memset(ws_sb[:].rearrange("p z c -> p (z c)").bitcast(I32), 0)
+        nc.gpsimd.memset(scales[:, 0:HALF].bitcast(I32), 0)
         for i in range(K_TILES):
-            (nc.vector if i < 2 else nc.gpsimd).memset(page[i][:], 0.0)
+            nc.gpsimd.memset(page[i][:], 0.0)
 
         def load_e(m):
             nc.sync.dma_start(e_sb[m][:], e_rows[m // PACK, m % PACK])
@@ -62,12 +60,13 @@ def tile_list_confidence_weighted_back_kernel(tc, e, pr, w_words, w_scales, run,
         def load_pr(m):
             nc.sync.dma_start(pr_sb[m][:], pr_rows[m // PACK, m % PACK])
 
-        load_pr(0)
         for m in range(PLANES):
-            if m + 1 < PLANES:
+            if m < PLANES - 1:
+                load_pr(m)
+            if m == PLANES - 2:
                 load_pr(m + 1)
             load_e(m)
-            if m == 0:
+            if m == 1:
                 for q in range(4):
                     nc.sync.dma_start(
                         ws_sb[32 * q : 32 * q + 4, :, :].bitcast(I32),
@@ -117,60 +116,46 @@ def tile_list_confidence_weighted_back_kernel(tc, e, pr, w_words, w_scales, run,
         dx = [keep.tile([P, J], F32, name="dx%d" % i) for i in range(1, K_TILES)]
         dx_first = [keep.tile([P, HALF], F32, name="dx0_%d" % h) for h in range(2)]
 
-        doubt = [keep.tile([P, J], F32, name="doubt%d" % m, tag="doubt%d" % m) for m in range(PLANES - 1)]
-        last_a = keep.tile([P, HALF], F32, name="last_a", tag="last_a")
-        last_b = keep.tile([P, HALF], F32, name="last_b")
-        d_first = keep.tile([P, PACK, J], F32, name="d_first")
-        pick(0)
-        fade(doubt[0][:], picked[0][:])
-        for m in range(PACK):
-            pick(m + 1)
-            fade(doubt[m + 1][:], picked[m + 1][:])
-            product(d_first[:, m, :], m, 0, J, doubt[m][:])
-
-        d_a = [keep.tile([P, 2, HALF], F32, name="d_a%d" % u) for u in range(2)]
-        woven_a = keep.tile([P, HALF, PACK], BF16, name="woven_a", align_bytes=64)
+        pieces = ((0, HALF), (HALF, HALF + QUARTER), (HALF + QUARTER, J))
+        doubt = [keep.tile([P, J], F32, name="doubt%d" % m) for m in range(PLANES - 1)]
+        last = [keep.tile([P, b - a], F32, name="last%d" % c, tag="slot%d" % (c + 1)) for c, (a, b) in enumerate(pieces)]
         woven_first = keep.tile([P, J, PACK], BF16, name="woven_first", align_bytes=64)
-        for r in range(PACK):
-            m = PACK + r
-            if m + 1 < PLANES - 1:
-                pick(m + 1)
-                fade(doubt[m + 1][:], picked[m + 1][:])
-            elif m + 1 == PLANES - 1:
-                pick(m + 1)
-                fade(last_a[:], picked[m + 1][:, 0:HALF])
-                fade(last_b[:], picked[m + 1][:, HALF:J])
-            product(d_a[r // 2][:, r % 2, :], m, 0, HALF, last_a[:] if m == PLANES - 1 else doubt[m][:, 0:HALF])
-            if r % 2 == 1:
-                weave_pair(woven_a, r - 1, d_a[r // 2][:])
-            if r == 0:
-                for h in range(2):
-                    nc.scalar.copy(
-                        woven_first[:, h * HALF : (h + 1) * HALF, :].rearrange("p (c i) r -> p c r i", i=4),
-                        d_first[:, :, h * HALF : (h + 1) * HALF].rearrange("p r (c i) -> p c r i", i=4),
-                    )
-                quantize(0, 0, woven_first)
-                multiply(early, 0, 0, 0)
-                for i in range(K_TILES):
-                    multiply(acc[i], i, 0, HALF)
-        quantize(1, 0, woven_a)
-        multiply(early, 0, 1, J)
-        nc.scalar.copy(dx_first[0][:], early[:, HALF:J])
+        woven = [keep.tile([P, b - a, PACK], BF16, name="woven%d" % a, align_bytes=64) for a, b in pieces]
 
-        d_low = keep.tile([P, 2, HALF], F32, name="d_low", tag="last_a")
-        woven_b = [keep.tile([P, QUARTER, PACK], BF16, name="woven_b%d" % c, align_bytes=64) for c in range(2)]
-        for r in range(2):
-            product(d_low[:, r, :], PACK + r, HALF, J, doubt[PACK + r][:, HALF:J])
-        for c in range(2):
-            weave_pair(woven_b[c], 0, d_low[:, :, c * QUARTER : (c + 1) * QUARTER])
-        for c in range(2):
-            a = HALF + c * QUARTER
-            d_high = keep.tile([P, 2, QUARTER], F32, name="d_high%d" % c, tag="doubt%d" % (PACK + c))
-            product(d_high[:, 0, :], PLANES - 2, a, a + QUARTER, doubt[PLANES - 2][:, a : a + QUARTER])
-            product(d_high[:, 1, :], PLANES - 1, a, a + QUARTER, last_b[:, c * QUARTER : (c + 1) * QUARTER])
-            weave_pair(woven_b[c], 2, d_high[:])
-        for c in range(2):
-            quantize(1, HALF + c * QUARTER, woven_b[c])
+        def plane_apart(m):
+            pick(m)
+            fade(doubt[m][:], picked[m][:])
+            errors = keep.tile([P, J], F32, name="errors%d" % m)
+            nc.vector.tensor_copy(errors[:], e_sb[m][:].indirect(offsets[:]))
+            if m < PACK:
+                nc.gpsimd.tensor_tensor(woven_first[:, :, m], errors[:], doubt[m][:], MULT)
+            else:
+                for c, (a, b) in enumerate(pieces):
+                    nc.gpsimd.tensor_tensor(woven[c][:, :, m - PACK], errors[:, a:b], doubt[m][:, a:b], MULT)
+
+        for m in range(PACK + 1):
+            plane_apart(m)
+        codes = keep.tile([P, HALF + PASSES * J], U32, name="codes", tag="e%d" % PACK, align_bytes=64)
+        quantize(0, 0, woven_first)
+        nc.gpsimd.memset(codes[:, 0:HALF], 0)
+        multiply(early, 0, 0, 0)
+        for i in range(K_TILES):
+            multiply(acc[i], i, 0, HALF)
+        plane_apart(PACK + 1)
+        pick(PLANES - 2)
+        fade(doubt[PLANES - 2][:], picked[PLANES - 2][:])
+        pick(PLANES - 1)
+        for c, (a, b) in enumerate(pieces):
+            fade(last[c][:], picked[PLANES - 1][:, a:b])
+        for c, (a, b) in enumerate(pieces):
+            d_high = keep.tile([P, 2, b - a], F32, name="d_high%d" % c, tag="slot%d" % c)
+            product(d_high[:, 0, :], PLANES - 2, a, b, doubt[PLANES - 2][:, a:b])
+            product(d_high[:, 1, :], PLANES - 1, a, b, last[c][:])
+            weave_pair(woven[c], 2, d_high[:])
+            quantize(1, a, woven[c])
+            if c == 0:
+                multiply(early, 0, 1, J)
+                nc.scalar.copy(dx_first[0][:], early[:, HALF:J])
         for i in range(K_TILES):
             multiply(acc[i], i, 1, HALF + J)
         nc.scalar.copy(dx_first[1][:], acc[0][:, HALF:J])

from contextlib import ExitStack

import concourse.mybir as mybir

N, K, T, J = 1024, 512, 1024, 512
FLOPS = 2 * N * K * J

F32 = mybir.dt.float32
BF16 = mybir.dt.bfloat16
I32 = mybir.dt.int32
U32 = mybir.dt.uint32
U16 = mybir.dt.uint16
U8 = mybir.dt.uint8
E5M2X4 = mybir.dt.float8_e5m2_x4
E2M1X4 = mybir.dt.float4_e2m1fn_x4
MULT = mybir.AluOpType.mult
ADD = mybir.AluOpType.add
SQUARE = mybir.ActivationFunctionType.Square

P = 128
PACK = 4
PASSES = N // (P * PACK)
PLANES = PASSES * PACK
K_TILES = K // P
LANES = 16
HALF = J // 2
QUARTER = J // 4


def tile_list_confidence_weighted_back_kernel(tc, e, pr, w_words, w_scales, run, offs, out):
    nc = tc.nc
    with ExitStack() as ctx:
        keep = ctx.enter_context(tc.tile_pool(name="keep", bufs=1))
        psum = ctx.enter_context(tc.psum_pool(name="psum", bufs=1))

        offsets = keep.tile([P, J // LANES], U16, name="offsets")
        nc.sync.dma_start(offsets[:], offs)

        def entries(a, b):
            return offsets[:, a // LANES : b // LANES]

        e_rows = e.rearrange("(z p r) t -> z r p t", p=P, r=PACK)
        pr_rows = pr.rearrange("(z p r) t -> z r p t", p=P, r=PACK)
        e_sb = [keep.tile([P, T], F32, name="e%d" % m, tag="e%d" % m, align_bytes=64) for m in range(PLANES)]
        pr_sb = [keep.tile([P, T], F32, name="pr%d" % m) for m in range(PLANES)]
        w_sb = [keep.tile([P, 2 * K], U8, name="w%d" % z, align_bytes=64) for z in range(PASSES)]
        ws_sb = keep.tile([P, PASSES, K], U8, name="ws", align_bytes=64)
        run_sb = [keep.tile([P, T], F32, name="run%d" % i) for i in range(K_TILES)]
        page = [keep.tile([P, T], F32, name="page%d" % i) for i in range(K_TILES)]
        scales = keep.tile([P, HALF + PASSES * J], U8, name="scales", align_bytes=64)

        nc.gpsimd.memset(ws_sb[:].rearrange("p z c -> p (z c)").bitcast(I32), 0)
        nc.gpsimd.memset(scales[:, 0:HALF].bitcast(I32), 0)
        for i in range(K_TILES):
            nc.gpsimd.memset(page[i][:], 0.0)

        def load_e(m):
            nc.sync.dma_start(e_sb[m][:], e_rows[m // PACK, m % PACK])

        def load_pr(m):
            nc.sync.dma_start(pr_sb[m][:], pr_rows[m // PACK, m % PACK])

        for m in range(PLANES):
            if m < PLANES - 1:
                load_pr(m)
            if m == PLANES - 2:
                load_pr(m + 1)
            load_e(m)
            if m == 1:
                for q in range(4):
                    nc.sync.dma_start(
                        ws_sb[32 * q : 32 * q + 4, :, :].bitcast(I32),
                        w_scales[:, 4 * q : 4 * q + 4, :].rearrange("z r c -> r z c").bitcast(I32),
                    )
            if m % PACK == PACK - 1:
                nc.sync.dma_start(w_sb[m // PACK][:].bitcast(I32), w_words[m // PACK].bitcast(I32))
        for i in range(K_TILES):
            nc.sync.dma_start(run_sb[i][:], run[i * P : (i + 1) * P, :])

        picked = [keep.tile([P, J], F32, name="picked%d" % m) for m in range(PLANES)]

        def pick(m):
            nc.vector.tensor_copy(picked[m][:], pr_sb[m][:].indirect(offsets[:]))

        def fade(dst, src):
            nc.scalar.activation(dst, src, SQUARE, bias=1.0, scale=-1.0)

        def product(dst, m, a, b, doubt):
            nc.vector.tensor_tensor(dst, e_sb[m][:].indirect(entries(a, b)), doubt, MULT)

        def weave_pair(woven, r, pair):
            nc.scalar.copy(woven[:, :, r : r + 2], pair.rearrange("p r j -> p j r"))

        def quantize(z, a, woven):
            c0 = HALF + z * J + a
            c1 = c0 + woven.shape[1]
            nc.vector.quantize_mx(
                out=codes[:, c0:c1].bitcast(E5M2X4),
                scales=scales[:, c0:c1],
                in_=woven[:].rearrange("p j r -> p (j r)"),
            )

        def multiply(dst, i, z, c0):
            nc.tensor.matmul_mx(
                out=dst[:],
                lhsT=w_sb[z][:, 2 * P * i : 2 * P * (i + 1)].bitcast(E2M1X4),
                lhsT_scale=ws_sb[:, z, P * i : P * (i + 1)],
                rhs=codes[:, c0 : c0 + J].bitcast(E5M2X4),
                rhs_scale=scales[:, c0 : c0 + J],
                start=(z == 0),
                stop=(z == PASSES - 1),
            )

        acc = [psum.tile([P, J], F32, name="acc%d" % i) for i in range(K_TILES)]
        early = psum.tile([P, J], F32, name="early")
        dx = [keep.tile([P, J], F32, name="dx%d" % i) for i in range(1, K_TILES)]
        dx_first = [keep.tile([P, HALF], F32, name="dx0_%d" % h) for h in range(2)]

        pieces = ((0, HALF), (HALF, HALF + QUARTER), (HALF + QUARTER, J))
        doubt = [keep.tile([P, J], F32, name="doubt%d" % m) for m in range(PLANES - 1)]
        last = [keep.tile([P, b - a], F32, name="last%d" % c, tag="slot%d" % (c + 1)) for c, (a, b) in enumerate(pieces)]
        woven_first = keep.tile([P, J, PACK], BF16, name="woven_first", align_bytes=64)
        woven = [keep.tile([P, b - a, PACK], BF16, name="woven%d" % a, align_bytes=64) for a, b in pieces]

        def plane_apart(m):
            pick(m)
            fade(doubt[m][:], picked[m][:])
            errors = keep.tile([P, J], F32, name="errors%d" % m)
            nc.vector.tensor_copy(errors[:], e_sb[m][:].indirect(offsets[:]))
            if m < PACK:
                nc.gpsimd.tensor_tensor(woven_first[:, :, m], errors[:], doubt[m][:], MULT)
            else:
                for c, (a, b) in enumerate(pieces):
                    nc.gpsimd.tensor_tensor(woven[c][:, :, m - PACK], errors[:, a:b], doubt[m][:, a:b], MULT)

        for m in range(PACK + 1):
            plane_apart(m)
        codes = keep.tile([P, HALF + PASSES * J], U32, name="codes", tag="e%d" % PACK, align_bytes=64)
        quantize(0, 0, woven_first)
        nc.gpsimd.memset(codes[:, 0:HALF], 0)
        multiply(early, 0, 0, 0)
        for i in range(K_TILES):
            multiply(acc[i], i, 0, HALF)
        plane_apart(PACK + 1)
        pick(PLANES - 2)
        fade(doubt[PLANES - 2][:], picked[PLANES - 2][:])
        pick(PLANES - 1)
        for c, (a, b) in enumerate(pieces):
            fade(last[c][:], picked[PLANES - 1][:, a:b])
        for c, (a, b) in enumerate(pieces):
            d_high = keep.tile([P, 2, b - a], F32, name="d_high%d" % c, tag="slot%d" % c)
            product(d_high[:, 0, :], PLANES - 2, a, b, doubt[PLANES - 2][:, a:b])
            product(d_high[:, 1, :], PLANES - 1, a, b, last[c][:])
            weave_pair(woven[c], 2, d_high[:])
            quantize(1, a, woven[c])
            if c == 0:
                multiply(early, 0, 1, J)
                nc.scalar.copy(dx_first[0][:], early[:, HALF:J])
        for i in range(K_TILES):
            multiply(acc[i], i, 1, HALF + J)
        nc.scalar.copy(dx_first[1][:], acc[0][:, HALF:J])
        for i in range(1, K_TILES):
            nc.scalar.copy(dx[i - 1][:], acc[i][:])

        for i in range(K_TILES):
            rows = slice(i * P, (i + 1) * P)
            if i == 0:
                for h in range(2):
                    nc.vector.tensor_copy(page[0][:].indirect(entries(h * HALF, (h + 1) * HALF)), dx_first[h][:])
            else:
                nc.vector.tensor_copy(page[i][:].indirect(offsets[:]), dx[i - 1][:])
            if i == K_TILES - 1:
                for h in range(2):
                    cols = slice(h * T // 2, (h + 1) * T // 2)
                    y_half = keep.tile([P, T // 2], F32, name="y_half%d" % h)
                    nc.vector.tensor_tensor(y_half[:], page[i][:, cols], run_sb[i][:, cols], ADD)
                    nc.sync.dma_start(out[rows, cols], y_half[:])
            else:
                y = keep.tile([P, T], F32, name="y%d" % i)
                nc.gpsimd.tensor_tensor(y[:], page[i][:], run_sb[i][:], ADD)
                nc.scalar.dma_start(out[rows, :], y[:])
